import numpy as np
import ml_dtypes


def mxq(x, axis, fmt="e4m3"):
    dtype, down = {"e4m3": (ml_dtypes.float8_e4m3fn, 7), "e5m2": (ml_dtypes.float8_e5m2, 14)}[fmt]
    v = np.moveaxis(np.asarray(x, np.float32).astype(ml_dtypes.bfloat16).astype(np.float64), axis, -1)
    blocks = v.reshape(v.shape[:-1] + (-1, 32))
    amax = np.abs(blocks).max(-1, keepdims=True)
    byte = np.maximum(np.where(amax > 0, np.frexp(amax)[1] - 1 + 127, 0) - down, 1)
    scale = np.exp2(byte - 127.0)
    codes = (blocks / scale).astype(np.float32).astype(dtype).astype(np.float64)
    return np.moveaxis((codes * scale).reshape(v.shape), -1, axis)


WIDE = False


def mx_kscale(k):
    if not WIDE:
        return np.ones(k)
    levels = np.array([10, -10, 5, -5, 0])
    if k % 512:
        return np.exp2(np.random.permutation(np.resize(levels, k // 32))).repeat(32)
    a = np.empty((k // 512, 16))
    for p in range(k // 512):
        a[p, :8] = np.random.permutation(np.resize(levels, 8))
        for g in range(8):
            far = levels[np.abs(levels - a[p, g]) >= 10]
            a[p, g + 8] = far[np.random.randint(len(far))]
    return np.exp2(a.ravel()).repeat(32)


def f64(x):
    return np.asarray(x).astype(np.float64)


def striped(idx):
    return np.tile(idx.reshape(-1, 16).T, (8, 1)).astype(np.uint16)


def unstriped(offs):
    return offs[:16].T.reshape(-1).astype(np.int64)


E2M1 = np.array([0.0, 0.5, 1.0, 1.5, 2.0, 3.0, 4.0, 6.0, -0.0, -0.5, -1.0, -1.5, -2.0, -3.0, -4.0, -6.0])


def pack_weight(w, fmt):
    k, n = w.shape
    w = f64(np.asarray(w, np.float32).astype(ml_dtypes.bfloat16)).reshape(k // 32, 32, n)
    amax = np.abs(w).max(1)
    if fmt == "e4m3":
        byte = np.frexp(amax)[1] - 1 + 127 - 7
    else:
        mant, ex = np.frexp(amax / 6.0)
        byte = np.where(mant > 0.5, ex, ex - 1) + 127
    byte = np.clip(np.where(amax > 0, byte, 1), 1, 254)
    scaled = (w * np.exp2(127.0 - byte)[:, None, :]).reshape(k, n).astype(np.float32)
    by_word = np.ascontiguousarray(scaled.reshape(k // 512, 128, 4, n).transpose(0, 1, 3, 2))
    if fmt == "e4m3":
        words = by_word.astype(ml_dtypes.float8_e4m3fn).view(np.uint8)
    else:
        c = by_word.astype(ml_dtypes.float4_e2m1fn).view(np.uint8) & 0xF
        words = (c[..., 0::2] | (c[..., 1::2] << 4)).reshape(k // 512, 128, 2 * n)
    return np.ascontiguousarray(words), np.ascontiguousarray(byte.astype(np.uint8).reshape(k // 512, 16, n))


def unpack_weight(words, scales, fmt):
    g, _, n = scales.shape
    words = np.ascontiguousarray(words).reshape(g, 128, n, -1)
    if fmt == "e4m3":
        vals = words.view(ml_dtypes.float8_e4m3fn).astype(np.float64)
    else:
        nib = np.empty((g, 128, n, 4), np.uint8)
        nib[..., 0::2] = words & 0xF
        nib[..., 1::2] = words >> 4
        vals = E2M1[nib]
    vals = vals * np.repeat(np.exp2(scales.astype(np.float64) - 127.0), 8, axis=1)[..., None]
    return vals.transpose(0, 1, 3, 2).reshape(g * 512, n)


def gelu(v):
    return 0.5 * v * (1.0 + np.tanh(np.sqrt(2.0 / np.pi) * (v + 0.044715 * v**3)))


def striped8(idx):
    return np.concatenate([v.reshape(-1, 16).T for v in idx]).astype(np.uint16)


def unstriped8(offs):
    return np.stack([offs[16 * g:16 * g + 16].T.reshape(-1) for g in range(8)]).astype(np.int64)


def heads(h, wgt, idx8):
    r = np.arange(h.shape[0])
    return wgt[r // 4 % 128] * h[r[:, None], idx8[r % 512 // 64]]


def put_heads(h, wgs, idx8, t2):
    r = np.arange(h.shape[0])
    page = np.zeros((h.shape[0], t2))
    page[r[:, None], idx8[r % 512 // 64]] = wgs[r // 4 % 128] * h
    return page


K, T, H, S, T2, P, N = 512, 4096, 1024, 1024, 2048, 1024, 384

def setup_inputs():
    n = np.random.standard_normal
    s = mx_kscale(K)[:, None]
    u = mx_kscale(H)[:, None]
    d = {}
    d["tab_words"], d["tab_scales"] = pack_weight(n((K, T)) * s, "e4m3")
    d["offs"] = striped(np.random.permutation(T)[:S])
    d["offs2"] = striped8(np.stack([np.random.permutation(T2)[:S] for _ in range(8)]))
    d["offs3"] = striped8(np.stack([np.random.permutation(T2)[:P] for _ in range(8)]))
    d["w1"] = (n((K, H)) / s * u.T / K**0.5).astype(np.float32)
    d["w2_words"], d["w2_scales"] = pack_weight(n((K, H)) / s * u.T / K**0.5, "e2m1")
    d["wgs"] = np.repeat(np.random.uniform(0.5, 2.0, (8, S)), 16, axis=0).astype(np.float32)
    d["wgt"] = np.repeat(np.random.uniform(0.5, 2.0, (8, P)), 16, axis=0).astype(np.float32)
    d["track"] = (n((H, P)) * u).astype(np.float32)
    d["w3"] = (n((K, N)) / s / K**0.5).astype(np.float32)
    d["w4_words"], d["w4_scales"] = pack_weight(n((H, N)) / u / H**0.5, "e4m3")
    return d

def reference(tab_words, tab_scales, offs, offs2, offs3, w1, w2_words, w2_scales, wgs, wgt, track, w3, w4_words, w4_scales):
    v = unpack_weight(tab_words, tab_scales, "e4m3")[:, unstriped(offs)]
    w2 = unpack_weight(w2_words, w2_scales, "e2m1")
    w4 = unpack_weight(w4_words, w4_scales, "e4m3")
    strike = mxq(f64(w1), 0, "e4m3").T @ v
    bend = w2.T @ v
    h = np.abs(strike) + bend
    page = put_heads(h, f64(wgs), unstriped8(offs2), T2)
    x = heads(page, f64(wgt), unstriped8(offs3))
    z = np.abs(x - f64(track))
    y = w4.T @ mxq(z, 0, "e4m3")
    b = mxq(f64(w3), 0, "e4m3").T @ v
    return y / (1.0 + np.square(b))

@@ -1,0 +1,346 @@
+from contextlib import ExitStack
+
+import concourse.mybir as mybir
+from concourse.masks import make_identity
+
+K, T, H, S, T2, NOUT = 512, 4096, 1024, 1024, 2048, 384
+FLOPS = 2 * K * H * S * 2 + 2 * H * NOUT * S + 2 * K * NOUT * S
+
+F32 = mybir.dt.float32
+BF16 = mybir.dt.bfloat16
+I32 = mybir.dt.int32
+U32 = mybir.dt.uint32
+U16 = mybir.dt.uint16
+U8 = mybir.dt.uint8
+FP8X4 = mybir.dt.float8_e4m3fn_x4
+FP4X4 = mybir.dt.float4_e2m1fn_x4
+ACT = mybir.ActivationFunctionType
+MULT = mybir.AluOpType.mult
+
+P = 128
+PACK = 4
+BANK = 512
+NBLK = S // P
+NT = NOUT // P
+PAGES = 2
+ADD = mybir.AluOpType.add
+FIRST_PIECES = [(0, 2), (2, 4), (4, 8)]
+EVEN_PIECES = [(0, 2), (2, 4), (4, 6), (6, 8)]
+TAIL_PIECES = [(0, 2), (2, 4), (4, 6), (6, 7), (7, 8)]
+
+
+def tile_list_wheel_flat_features_kernel(
+    tc, tab_words, tab_scales, offs, offs2, offs3, w1, w2_words, w2_scales, wgs, wgt, track, w3, w4_words, w4_scales, out
+):
+    nc = tc.nc
+    with ExitStack() as ctx:
+        lists = ctx.enter_context(tc.tile_pool(name="lists", bufs=1))
+        keep = ctx.enter_context(tc.tile_pool(name="keep", bufs=1))
+        ring = ctx.enter_context(tc.tile_pool(name="ring", bufs=2))
+        psum = ctx.enter_context(tc.psum_pool(name="psum", bufs=1))
+
+        def slot(tag, shape, dtype, name):
+            return keep.tile(shape, dtype, name=name, tag=tag, align_bytes=64)
+
+        turn = {"mm": 0, "tr": 0}
+
+        def bank_tile(kind, shape, name, index=None):
+            if index is None:
+                index = turn[kind] % 4 + (0 if kind == "mm" else 4)
+                turn[kind] = turn[kind] + 1
+            return psum.tile(shape, F32, name=name, tag="bank%d" % index)
+
+        idx = lists.tile([P, S // 16], U16, name="idx")
+        idx2 = lists.tile([P, S // 16], U16, name="idx2")
+        idx3 = lists.tile([P, S // 16], U16, name="idx3")
+
+        tabs = slot("row0", [P, T], U8, "tabs")
+        vw = [slot("vw%d" % i, [P, BANK], U32, "vw") for i in range(2)]
+        vs = slot("vs", [P, S], U8, "vs")
+        w2w_raw = slot("row1", [P, 2 * H], U8, "w2w_raw")
+        w2s_raw = slot("w2s_raw", [P, H], U8, "w2s_raw")
+        w2w = slot("w2w", [P, 2 * H], U8, "w2w")
+        w2s = slot("w2s", [P, H], U8, "w2s")
+        w1b = [slot("w1b%d" % b, [P, PACK, BANK], BF16, "w1b") for b in range(2)]
+        w1c = slot("w1c", [P, H], U32, "w1c")
+        w1s = slot("w1s", [P, H], U8, "w1s")
+        w3b = slot("w3b", [P, NOUT * PACK], BF16, "w3b")
+        w3c = slot("w3c", [P, NOUT], U32, "w3c")
+        w3s = slot("w3s", [P, NOUT], U8, "w3s")
+        pages = {i: slot("page%d" % i, [P, T2], F32, "page") for i in range(1)}
+        zc = [slot("zc%d" % b, [P, S], U32, "zc") for b in range(2)]
+        zs = [slot("zs%d" % b, [P, S], U8, "zs") for b in range(2)]
+        damp = slot("damp", [P, NT, S], F32, "damp")
+        ident = slot("ident", [P, P], F32, "ident")
+
+        w1v = w1.rearrange("(p i) r -> p i r", i=PACK)
+        trackv = track.rearrange("(b p t) j -> b p t j", b=2, t=PACK)
+        outv = out.rearrange("(n p) j -> p n j", p=P)
+
+        nc.sync.dma_start(idx[:], offs)
+        nc.sync.dma_start(idx2[:], offs2)
+        nc.sync.dma_start(idx3[:], offs3)
+        nc.sync.dma_start(w2w_raw[:].bitcast(I32), w2_words[0].bitcast(I32))
+        w1raw = {}
+
+        def load_w1(b, tag):
+            w1raw[b] = slot(tag, [P, PACK, BANK], F32, "w1raw")
+            nc.sync.dma_start(w1raw[b][:], w1v[:, :, b * BANK : (b + 1) * BANK])
+
+        load_w1(0, "wraw")
+        nc.vector.memset(tabs[:].bitcast(I32), 0)
+        for q in range(4):
+            nc.sync.dma_start(tabs[32 * q : 32 * q + 4, :].bitcast(I32), tab_scales[0, 4 * q : 4 * q + 4, :].bitcast(I32))
+        ident_first = slot("big0", [P, P], F32, "ident_first")
+        make_identity(nc, ident_first[:])
+        nc.gpsimd.memset(w2s_raw[:].bitcast(I32), 0)
+        for q in range(4):
+            nc.gpsimd.dma_start(w2s_raw[32 * q : 32 * q + 4, :].bitcast(I32), w2_scales[0, 4 * q : 4 * q + 4, :].bitcast(I32))
+        nc.vector.tensor_copy(ident[:], ident_first[:])
+        tabw = slot("big0", [P, T], I32, "tabw")
+        nc.sync.dma_start(tabw[:], tab_words[0].rearrange("p t i -> p (t i)").bitcast(I32))
+        nc.vector.memset(pages[0][:], 0.0)
+
+        def deal_w2(b):
+            words = slice(2 * BANK * b, 2 * BANK * (b + 1))
+            nc.vector.tensor_copy(
+                w2w[:, words].bitcast(U16).rearrange("p (t q) -> p t q", t=PACK), w2w_raw[:, words].bitcast(U16).rearrange("p (q t) -> p t q", t=PACK)
+            )
+
+        def deal_w2_scales(b):
+            cols = slice(BANK * b, BANK * (b + 1))
+            nc.vector.tensor_copy(w2s[:, cols].rearrange("p (t q) -> p t q", t=PACK), w2s_raw[:, cols].rearrange("p (q t) -> p t q", t=PACK))
+
+        deal_w2(0)
+        deal_w2(1)
+        wgs_sb = slot("row1", [P, S], F32, "wgs_sb")
+        nc.sync.dma_start(wgs_sb[:], wgs)
+        nc.vector.tensor_copy(vs[:], tabs[:].indirect(idx[:]))
+        deal_w2_scales(0)
+        wgt_sb = slot("row0", [P, S], F32, "wgt_sb")
+        nc.sync.dma_start(wgt_sb[:], wgt)
+
+        def v_block(c):
+            return vw[c // 4][:, (c % 4) * P : (c % 4 + 1) * P].bitcast(FP8X4), vs[:, c * P : (c + 1) * P]
+
+        def quantize_w1(b, t0, t1):
+            cols = slice(b * BANK + t0 * P, b * BANK + t1 * P)
+            nc.vector.quantize_mx(
+                out=w1c[:, cols].bitcast(FP8X4), scales=w1s[:, cols], in_=w1b[b][:, t0:t1, :].rearrange("p t m -> p (t m)")
+            )
+
+        def cast_w1(copy, b, ts, qs):
+            src = w1raw[b][:].rearrange("p i (q t) -> p q t i", t=PACK)[:, qs, ts, :]
+            dst = w1b[b][:].rearrange("p t (q i) -> p q t i", i=PACK)[:, qs, ts, :]
+            copy(dst, src)
+
+        h_tiles = {}
+        first_tenants = {
+            (0, 0): ("page1", None),
+            (0, 4): ("wgt_neg", None),
+            (1, 0): ("late", None),
+            (2, 0): ("big1", "w4w"),
+            (2, 4): ("w4s", None),
+        }
+
+        def staging(tag, n, name):
+            if tag is None:
+                return ring.tile([P, n, P], F32, name=name, tag=name)
+            return slot(tag, [P, n, P], F32, name)
+
+        def make_h(s, c0, c1):
+            n = c1 - c0
+            if c0 == 0:
+                h_tiles[s] = ring.tile([P, S], F32, name="h", tag="h", bufs=3)
+            tags = first_tenants.get((s, c0), (None, None))
+            cols = slice(s * P, (s + 1) * P)
+            strike_bank = bank_tile("mm", [P, n, P], "strike_bank")
+            bend_bank = bank_tile("mm", [P, n, P], "bend_bank")
+            for cc in range(n):
+                codes, scales = v_block(c0 + cc)
+                nc.tensor.matmul_mx(
+                    out=strike_bank[:, cc, :], lhsT=codes, lhsT_scale=scales,
+                    rhs=w1c[:, cols].bitcast(FP8X4), rhs_scale=w1s[:, cols], start=True, stop=True,
+                )
+            for cc in range(n):
+                codes, scales = v_block(c0 + cc)
+                nc.tensor.matmul_mx(
+                    out=bend_bank[:, cc, :], lhsT=codes, lhsT_scale=scales,
+                    rhs=w2w[:, 2 * P * s : 2 * P * (s + 1)].bitcast(FP4X4), rhs_scale=w2s[:, cols], start=True, stop=True,
+                )
+            strikeT = staging(tags[0], n, "strikeT")
+            nc.scalar.activation(strikeT[:], strike_bank[:], ACT.Abs)
+            bendT = staging(tags[1], n, "bendT")
+            nc.scalar.copy(bendT[:], bend_bank[:])
+            hb = bank_tile("tr", [P, n, P], "h_bank")
+            for cc in range(n):
+                nc.tensor.matmul(hb[:, cc, :], strikeT[:, cc, :], ident[:], start=(cc == 0), stop=False, is_transpose=True)
+            for cc in range(n):
+                nc.tensor.matmul(hb[:, cc, :], bendT[:, cc, :], ident[:], start=False, stop=(cc == n - 1), is_transpose=True)
+            nc.scalar.copy(h_tiles[s][:, c0 * P : c1 * P], hb[:].rearrange("p c j -> p (c j)"))
+
+        def put_h(s, c0, c1):
+            cols = slice(c0 * P, c1 * P)
+            nc.vector.tensor_tensor(pages[s % PAGES][:].indirect(idx2[:, c0 * P // 16 : c1 * P // 16]), h_tiles[s][:, cols], wgs_sb[:, cols], MULT)
+
+        x_tiles = {}
+
+        def pick_x(s, dst, c0, c1):
+            cols = slice(c0 * P, c1 * P)
+            nc.vector.tensor_tensor(dst, pages[s % PAGES][:].indirect(idx3[:, c0 * P // 16 : c1 * P // 16]), wgt_neg[:, cols], MULT)
+
+        track_tiles = {}
+
+        def load_track(b):
+            track_tiles[b] = slot("big%d" % b, [P, PACK, S], F32, "track_sb")
+            nc.sync.dma_start(track_tiles[b][:], trackv[b])
+
+        zT = {}
+
+        def distance(b, u, c0, c1, slices):
+            n = c1 - c0
+            bank = bank_tile("tr", [P, n, slices, P], "d_bank")
+            slots = [(cc, e) for e in range(slices) for cc in range(n)]
+            for m, (cc, e) in enumerate(slots):
+                cols = slice((c0 + cc) * P, (c0 + cc + 1) * P)
+                nc.tensor.matmul(bank[:, cc, e, :], track_tiles[b][:, 2 * u + e, cols], ident[:], start=(m == 0), stop=False, is_transpose=True)
+            for m, (cc, e) in enumerate(slots):
+                cols = slice((c0 + cc) * P, (c0 + cc + 1) * P)
+                nc.tensor.matmul(
+                    bank[:, cc, e, :], x_tiles[PACK * b + 2 * u + e][:, cols], ident[:], start=False, stop=(m == len(slots) - 1), is_transpose=True
+                )
+            zt = ring.tile([P, n * 2 * P], BF16, name="zT", tag="zT%d" % u, bufs=5)
+            src = bank[:].rearrange("j c e p -> j c p e")
+            if slices == 1:
+                src = src.to_broadcast([P, n, P, 2])
+            nc.scalar.activation(zt[:].rearrange("j (c p e) -> j c p e", c=n, e=2), src, ACT.Abs)
+            zT[(b, u, c0)] = zt
+
+        def turn_back(b, c0, c1):
+            n = c1 - c0
+            bank = bank_tile("tr", [P, n, 2, P], "w_bank")
+            for u in range(2):
+                words = zT[(b, u, c0)][:].bitcast(F32)
+                for cc in range(n):
+                    nc.tensor.transpose(bank[:, cc, u, :], words[:, cc * P : (cc + 1) * P], ident[:])
+            zq = ring.tile([P, n * P * PACK], BF16, name="zq", tag="zq", bufs=5, align_bytes=64)
+            nc.scalar.copy(zq[:].bitcast(F32).rearrange("p (c j u) -> p c j u", c=n, u=2), bank[:].rearrange("p c u j -> p c j u"))
+            return zq
+
+        def quantize_z(b, zq, c0, c1):
+            cols = slice(c0 * P, c1 * P)
+            nc.vector.quantize_mx(out=zc[b][:, cols].bitcast(FP8X4), scales=zs[b][:, cols], in_=zq[:])
+
+        def prepare_w3():
+            raw = slot("late", [P, PACK, NOUT], F32, "w3raw")
+            nc.sync.dma_start(raw[:], w3.rearrange("(p i) n -> p i n", i=PACK))
+            for n in range(NT):
+                cols = slice(n * P, (n + 1) * P)
+                nc.scalar.copy(w3b[:].rearrange("p (n i) -> p n i", i=PACK)[:, cols, :], raw[:].rearrange("p i n -> p n i")[:, cols, :])
+            for c0, c1 in ((0, 256), (256, NOUT)):
+                nc.vector.quantize_mx(out=w3c[:, c0:c1].bitcast(FP8X4), scales=w3s[:, c0:c1], in_=w3b[:, PACK * c0 : PACK * c1])
+
+        def damping(n):
+            cols = slice(n * P, (n + 1) * P)
+            for half in range(2):
+                bank = bank_tile("mm", [P, BANK], "b_bank")
+                nc.tensor.matmul_mx(
+                    out=bank[:], lhsT=w3c[:, cols].bitcast(FP8X4), lhsT_scale=w3s[:, cols],
+                    rhs=vw[half][:].bitcast(FP8X4), rhs_scale=vs[:, half * BANK : (half + 1) * BANK], start=True, stop=True,
+                )
+                nc.scalar.activation(damp[:, n, half * BANK : (half + 1) * BANK], bank[:], ACT.Square)
+            nc.scalar.activation(damp[:, n, :], damp[:, n, :], ACT.Abs_reciprocal_sqrt, bias=1.0)
+            nc.scalar.activation(damp[:, n, :], damp[:, n, :], ACT.Square)
+
+        def y_passes(bank, a, n0, n1, c0, c1):
+            cols = slice(c0 * P, c1 * P)
+            for n in range(n0, n1):
+                nc.tensor.matmul_mx(
+                    out=bank[:, n - n0, :], lhsT=w4w[:, a, n * P : (n + 1) * P].bitcast(FP8X4), lhsT_scale=w4s[:, a, n * P : (n + 1) * P],
+                    rhs=zc[a][:, cols].bitcast(FP8X4), rhs_scale=zs[a][:, cols], start=(a == 0 and n == n0), stop=(a == 1 and n == n1 - 1),
+                )
+
+        cast_w1(nc.scalar.copy, 0, slice(0, PACK), slice(0, P))
+        quantize_w1(0, 0, PACK)
+        for half in range(2):
+            nc.vector.tensor_copy(vw[half][:], tabw[:].bitcast(U32).indirect(idx[:, 32 * half : 32 * half + 32]))
+        deal_w2_scales(1)
+        for c0, c1 in FIRST_PIECES:
+            make_h(0, c0, c1)
+        make_h(1, 0, 4)
+        make_h(1, 4, NBLK)
+        wgt_neg = slot("wgt_neg", [P, S], F32, "wgt_neg")
+        nc.scalar.activation(wgt_neg[:], wgt_sb[:], ACT.Copy, scale=-1.0)
+        for i in range(1, PAGES):
+            pages[i] = slot("page%d" % i, [P, T2], F32, "page")
+            nc.gpsimd.memset(pages[i][:], 0.0)
+        load_track(0)
+
+        last = 2 * PACK - 1
+        for s in range(last):
+            b, t = divmod(s, PACK)
+            if s + 2 <= last:
+                make_h(s + 2, 0, 4)
+                make_h(s + 2, 4, NBLK)
+            if s == 0:
+                prepare_w3()
+            if s == 1:
+                load_w1(1, "late")
+                for q0 in range(0, P, 32):
+                    cast_w1(nc.scalar.copy, 1, slice(0, PACK), slice(q0, q0 + 32))
+                quantize_w1(1, 0, PACK)
+                load_track(1)
+                w4w = slot("w4w", [P, 2, NOUT], I32, "w4w")
+                w4s = slot("w4s", [P, 2, NOUT], U8, "w4s")
+                nc.gpsimd.memset(w4s[:].rearrange("p a n -> p (a n)").bitcast(I32), 0)
+                nc.sync.dma_start(w4w[:], w4_words.rearrange("a p n i -> p a (n i)").bitcast(I32))
+                for q in range(4):
+                    nc.sync.dma_start(
+                        w4s[32 * q : 32 * q + 4, :, :].bitcast(I32), w4_scales[:, 4 * q : 4 * q + 4, :].rearrange("a r n -> r a n").bitcast(I32)
+                    )
+            if 2 <= s < 2 + NT:
+                damping(s - 2)
+            for c0, c1 in FIRST_PIECES if s == 0 else [(0, NBLK)]:
+                put_h(s, c0, c1)
+            x_tiles[s] = ring.tile([P, S], F32, name="xneg", tag="xneg", bufs=4)
+            pick_x(s, x_tiles[s][:], 0, NBLK)
+            pieces = EVEN_PIECES if b == 0 else TAIL_PIECES
+            if t % 2 == 1:
+                for c0, c1 in pieces:
+                    distance(b, t // 2, c0, c1, 2)
+                    if t == PACK - 1:
+                        quantize_z(b, turn_back(b, c0, c1), c0, c1)
+
+        zq_tail = {}
+        for c0, c1 in TAIL_PIECES:
+            distance(1, 1, c0, c1, 1)
+            zq_tail[c0] = turn_back(1, c0, c1)
+        put_h(last, 0, NBLK)
+        y_banks = {}
+        index = 0
+        for c0, c1 in TAIL_PIECES:
+            width = (c1 - c0) * P
+            per_bank = BANK // width
+            y_banks[c0] = []
+            for n0 in range(0, NT, per_bank):
+                n1 = min(NT, n0 + per_bank)
+                bank = bank_tile("mm", [P, n1 - n0, width], "y_bank", index)
+                index = index + 1
+                y_passes(bank, 0, n0, n1, c0, c1)
+                y_banks[c0].append((bank, n0, n1))
+        for c0, c1 in TAIL_PIECES:
+            cols = slice(c0 * P, c1 * P)
+            width = (c1 - c0) * P
+            xl = ring.tile([P, width], F32, name="x_last", tag="x_last", bufs=5)
+            pick_x(last, xl[:], c0, c1)
+            dl = ring.tile([P, width], F32, name="d_last", tag="d_last", bufs=5)
+            nc.vector.tensor_tensor(dl[:], xl[:], track_tiles[1][:, PACK - 1, cols], ADD)
+            nc.scalar.activation(zq_tail[c0][:].rearrange("p (j t) -> p j t", t=PACK)[:, :, PACK - 1], dl[:], ACT.Abs)
+        for c0, c1 in TAIL_PIECES:
+            cols = slice(c0 * P, c1 * P)
+            quantize_z(1, zq_tail[c0], c0, c1)
+            res = ring.tile([P, NT, (c1 - c0) * P], F32, name="res", tag="res", bufs=5)
+            for bank, n0, n1 in y_banks[c0]:
+                y_passes(bank, 1, n0, n1, c0, c1)
+                nc.vector.tensor_tensor(res[:, n0:n1, :], bank[:], damp[:, n0:n1, cols], MULT)
+            nc.sync.dma_start(outv[:, :, cols], res[:])

@@ -22,9 +22,11 @@ PACK = 4
 BANK = 512
 NBLK = S // P
 NT = NOUT // P
-PAGES = 2
+PAGES = 3
+AHEAD = 3
 ADD = mybir.AluOpType.add
 FIRST_PIECES = [(0, 2), (2, 4), (4, 8)]
+Y_BANKS = (0, 1, 2, 3, 7, 4, 5, 6)
 EVEN_PIECES = [(0, 2), (2, 4), (4, 6), (6, 8)]
 TAIL_PIECES = [(0, 2), (2, 4), (4, 6), (6, 7), (7, 8)]
 
@@ -42,11 +44,12 @@ def tile_list_wheel_flat_features_kernel(
         def slot(tag, shape, dtype, name):
             return keep.tile(shape, dtype, name=name, tag=tag, align_bytes=64)
 
-        turn = {"mm": 0, "tr": 0}
+        bank_sets = {"mm": (0, 1, 2, 3), "h": (4, 5), "z": (6, 7), "d_tail": (4, 5), "w_tail": (6, 7, 4, 5)}
+        turn = {kind: 0 for kind in bank_sets}
 
         def bank_tile(kind, shape, name, index=None):
             if index is None:
-                index = turn[kind] % 4 + (0 if kind == "mm" else 4)
+                index = bank_sets[kind][turn[kind] % len(bank_sets[kind])]
                 turn[kind] = turn[kind] + 1
             return psum.tile(shape, F32, name=name, tag="bank%d" % index)
 
@@ -55,7 +58,6 @@ def tile_list_wheel_flat_features_kernel(
         idx3 = lists.tile([P, S // 16], U16, name="idx3")
 
         tabs = slot("row0", [P, T], U8, "tabs")
-        vw = [slot("vw%d" % i, [P, BANK], U32, "vw") for i in range(2)]
         vs = slot("vs", [P, S], U8, "vs")
         w2w_raw = slot("row1", [P, 2 * H], U8, "w2w_raw")
         w2s_raw = slot("w2s_raw", [P, H], U8, "w2s_raw")
@@ -136,22 +138,24 @@ def tile_list_wheel_flat_features_kernel(
 
         h_tiles = {}
         first_tenants = {
-            (0, 0): ("page1", None),
-            (0, 4): ("wgt_neg", None),
-            (1, 0): ("late", None),
+            (0, 2): ("page1", None),
+            (0, 4): ("wgt_neg", "page2"),
             (2, 0): ("big1", "w4w"),
             (2, 4): ("w4s", None),
         }
+        for s in range(1, 4):
+            first_tenants[(s + 2, 4)] = ("x%d" % s, None)
+        first_tenants[(6, 4)] = ("x4", "x5")
 
         def staging(tag, n, name):
             if tag is None:
                 return ring.tile([P, n, P], F32, name=name, tag=name)
             return slot(tag, [P, n, P], F32, name)
 
-        def make_h(s, c0, c1):
+        h_banks = {}
+
+        def sum_h(s, c0, c1):
             n = c1 - c0
-            if c0 == 0:
-                h_tiles[s] = ring.tile([P, S], F32, name="h", tag="h", bufs=3)
             tags = first_tenants.get((s, c0), (None, None))
             cols = slice(s * P, (s + 1) * P)
             strike_bank = bank_tile("mm", [P, n, P], "strike_bank")
@@ -172,12 +176,41 @@ def tile_list_wheel_flat_features_kernel(
             nc.scalar.activation(strikeT[:], strike_bank[:], ACT.Abs)
             bendT = staging(tags[1], n, "bendT")
             nc.scalar.copy(bendT[:], bend_bank[:])
-            hb = bank_tile("tr", [P, n, P], "h_bank")
+            hb = bank_tile("h", [P, n, P], "h_bank")
             for cc in range(n):
                 nc.tensor.matmul(hb[:, cc, :], strikeT[:, cc, :], ident[:], start=(cc == 0), stop=False, is_transpose=True)
             for cc in range(n):
                 nc.tensor.matmul(hb[:, cc, :], bendT[:, cc, :], ident[:], start=False, stop=(cc == n - 1), is_transpose=True)
-            nc.scalar.copy(h_tiles[s][:, c0 * P : c1 * P], hb[:].rearrange("p c j -> p (c j)"))
+            h_banks[(s, c0)] = hb
+
+        def copy_h(s, c0, c1):
+            if c0 == 0 and s < 6:
+                h_tiles[s] = ring.tile([P, S], F32, name="h", tag="h", bufs=AHEAD + 1)
+            if c0 == 0 and s >= 6:
+                h_tiles[s] = slot("h_last", [P, S], F32, "h")
+            nc.scalar.copy(h_tiles[s][:, c0 * P : c1 * P], h_banks[(s, c0)][:].rearrange("p c j -> p (c j)"))
+
+        def make_h(s, c0, c1):
+            sum_h(s, c0, c1)
+            copy_h(s, c0, c1)
+
+        def make_h_direct(s, c0, c1):
+            rows = slice(s * P, (s + 1) * P)
+            cols = slice(c0 * P, c1 * P)
+            width = (c1 - c0) * P
+            strike_bank = bank_tile("mm", [P, width], "strike_bank")
+            bend_bank = bank_tile("mm", [P, width], "bend_bank")
+            nc.tensor.matmul_mx(
+                out=strike_bank[:], lhsT=w1c[:, rows].bitcast(FP8X4), lhsT_scale=w1s[:, rows],
+                rhs=vw[0][:, cols].bitcast(FP8X4), rhs_scale=vs[:, cols], start=True, stop=True,
+            )
+            nc.tensor.matmul_mx(
+                out=bend_bank[:], lhsT=w2w[:, 2 * P * s : 2 * P * (s + 1)].bitcast(FP4X4), lhsT_scale=w2s[:, rows],
+                rhs=vw[0][:, cols].bitcast(FP8X4), rhs_scale=vs[:, cols], start=True, stop=True,
+            )
+            strike = slot("late", [P, width], F32, "strike")
+            nc.scalar.activation(strike[:], strike_bank[:], ACT.Abs)
+            nc.vector.tensor_tensor(h_tiles[s][:, cols], bend_bank[:], strike[:], ADD)
 
         def put_h(s, c0, c1):
             cols = slice(c0 * P, c1 * P)
@@ -197,9 +230,9 @@ def tile_list_wheel_flat_features_kernel(
 
         zT = {}
 
-        def distance(b, u, c0, c1, slices):
+        def distance(b, u, c0, c1, slices, kind):
             n = c1 - c0
-            bank = bank_tile("tr", [P, n, slices, P], "d_bank")
+            bank = bank_tile(kind, [P, n, slices, P], "d_bank")
             slots = [(cc, e) for e in range(slices) for cc in range(n)]
             for m, (cc, e) in enumerate(slots):
                 cols = slice((c0 + cc) * P, (c0 + cc + 1) * P)
@@ -209,20 +242,20 @@ def tile_list_wheel_flat_features_kernel(
                 nc.tensor.matmul(
                     bank[:, cc, e, :], x_tiles[PACK * b + 2 * u + e][:, cols], ident[:], start=False, stop=(m == len(slots) - 1), is_transpose=True
                 )
-            zt = ring.tile([P, n * 2 * P], BF16, name="zT", tag="zT%d" % u, bufs=5)
+            zt = ring.tile([P, n * 2 * P], BF16, name="zT", tag="zT%d%d" % (u, slices), bufs=(4 if slices == 2 else 2))
             src = bank[:].rearrange("j c e p -> j c p e")
             if slices == 1:
                 src = src.to_broadcast([P, n, P, 2])
             nc.scalar.activation(zt[:].rearrange("j (c p e) -> j c p e", c=n, e=2), src, ACT.Abs)
-            zT[(b, u, c0)] = zt
+            for cc in range(n):
+                zT[(b, u, c0 + cc)] = zt[:].bitcast(F32)[:, cc * P : (cc + 1) * P]
 
-        def turn_back(b, c0, c1):
+        def turn_back(b, c0, c1, kind):
             n = c1 - c0
-            bank = bank_tile("tr", [P, n, 2, P], "w_bank")
+            bank = bank_tile(kind, [P, n, 2, P], "w_bank")
             for u in range(2):
-                words = zT[(b, u, c0)][:].bitcast(F32)
                 for cc in range(n):
-                    nc.tensor.transpose(bank[:, cc, u, :], words[:, cc * P : (cc + 1) * P], ident[:])
+                    nc.tensor.transpose(bank[:, cc, u, :], zT[(b, u, c0 + cc)], ident[:])
             zq = ring.tile([P, n * P * PACK], BF16, name="zq", tag="zq", bufs=5, align_bytes=64)
             nc.scalar.copy(zq[:].bitcast(F32).rearrange("p (c j u) -> p c j u", c=n, u=2), bank[:].rearrange("p c u j -> p c j u"))
             return zq
@@ -262,10 +295,13 @@ def tile_list_wheel_flat_features_kernel(
 
         cast_w1(nc.scalar.copy, 0, slice(0, PACK), slice(0, P))
         quantize_w1(0, 0, PACK)
+        deal_w2_scales(1)
+        vw = [slot(tag, [P, BANK], U32, "vw") for tag in ("w1b0", "w2s_raw")]
         for half in range(2):
             nc.vector.tensor_copy(vw[half][:], tabw[:].bitcast(U32).indirect(idx[:, 32 * half : 32 * half + 32]))
-        deal_w2_scales(1)
-        for c0, c1 in FIRST_PIECES:
+        h_tiles[0] = ring.tile([P, S], F32, name="h", tag="h", bufs=AHEAD + 1)
+        make_h_direct(0, *FIRST_PIECES[0])
+        for c0, c1 in FIRST_PIECES[1:]:
             make_h(0, c0, c1)
         make_h(1, 0, 4)
         make_h(1, 4, NBLK)
@@ -277,18 +313,25 @@ def tile_list_wheel_flat_features_kernel(
         load_track(0)
 
         last = 2 * PACK - 1
+        load_w1(1, "late")
+        for q0 in range(0, P, 32):
+            cast_w1(nc.scalar.copy, 1, slice(0, PACK), slice(q0, q0 + 32))
+        quantize_w1(1, 0, PACK)
+        for s in range(2, AHEAD):
+            make_h(s, 0, 4)
+            make_h(s, 4, NBLK)
+        for c0, c1 in FIRST_PIECES:
+            put_h(0, c0, c1)
         for s in range(last):
             b, t = divmod(s, PACK)
-            if s + 2 <= last:
-                make_h(s + 2, 0, 4)
-                make_h(s + 2, 4, NBLK)
-            if s == 0:
-                prepare_w3()
+            if s + AHEAD < last:
+                make_h(s + AHEAD, 0, 4)
+                make_h(s + AHEAD, 4, NBLK)
+            if s + AHEAD == last:
+                sum_h(last, 0, 4)
+                sum_h(last, 4, NBLK)
             if s == 1:
-                load_w1(1, "late")
-                for q0 in range(0, P, 32):
-                    cast_w1(nc.scalar.copy, 1, slice(0, PACK), slice(q0, q0 + 32))
-                quantize_w1(1, 0, PACK)
+                prepare_w3()
                 load_track(1)
                 w4w = slot("w4w", [P, 2, NOUT], I32, "w4w")
                 w4s = slot("w4s", [P, 2, NOUT], U8, "w4s")
@@ -300,21 +343,27 @@ def tile_list_wheel_flat_features_kernel(
                     )
             if 2 <= s < 2 + NT:
                 damping(s - 2)
-            for c0, c1 in FIRST_PIECES if s == 0 else [(0, NBLK)]:
-                put_h(s, c0, c1)
-            x_tiles[s] = ring.tile([P, S], F32, name="xneg", tag="xneg", bufs=4)
+            if s == 1:
+                put_h(1, 0, NBLK)
+            if 1 <= s < last - 2:
+                put_h(s + 1, 0, NBLK)
+            if s == last - 1:
+                put_h(s, 0, NBLK)
+                copy_h(last, 0, 4)
+                copy_h(last, 4, NBLK)
+            x_tiles[s] = slot("x%d" % s, [P, S], F32, "xneg")
             pick_x(s, x_tiles[s][:], 0, NBLK)
-            pieces = EVEN_PIECES if b == 0 else TAIL_PIECES
             if t % 2 == 1:
-                for c0, c1 in pieces:
-                    distance(b, t // 2, c0, c1, 2)
+                for c0, c1 in EVEN_PIECES:
+                    distance(b, t // 2, c0, c1, 2, "z")
                     if t == PACK - 1:
-                        quantize_z(b, turn_back(b, c0, c1), c0, c1)
+                        quantize_z(b, turn_back(b, c0, c1, "z"), c0, c1)
 
         zq_tail = {}
+        distance(1, 1, 0, 4, 1, "d_tail")
+        distance(1, 1, 4, NBLK, 1, "d_tail")
         for c0, c1 in TAIL_PIECES:
-            distance(1, 1, c0, c1, 1)
-            zq_tail[c0] = turn_back(1, c0, c1)
+            zq_tail[c0] = turn_back(1, c0, c1, "w_tail")
         put_h(last, 0, NBLK)
         y_banks = {}
         index = 0
@@ -324,7 +373,7 @@ def tile_list_wheel_flat_features_kernel(
             y_banks[c0] = []
             for n0 in range(0, NT, per_bank):
                 n1 = min(NT, n0 + per_bank)
-                bank = bank_tile("mm", [P, n1 - n0, width], "y_bank", index)
+                bank = bank_tile("mm", [P, n1 - n0, width], "y_bank", Y_BANKS[index])
                 index = index + 1
                 y_passes(bank, 0, n0, n1, c0, c1)
                 y_banks[c0].append((bank, n0, n1))
@@ -339,7 +388,7 @@ def tile_list_wheel_flat_features_kernel(
         for c0, c1 in TAIL_PIECES:
             cols = slice(c0 * P, c1 * P)
             quantize_z(1, zq_tail[c0], c0, c1)
-            res = ring.tile([P, NT, (c1 - c0) * P], F32, name="res", tag="res", bufs=5)
+            res = ring.tile([P, NT, (c1 - c0) * P], F32, name="res", tag="res", bufs=4)
             for bank, n0, n1 in y_banks[c0]:
                 y_passes(bank, 1, n0, n1, c0, c1)
                 nc.vector.tensor_tensor(res[:, n0:n1, :], bank[:], damp[:, n0:n1, cols], MULT)

from contextlib import ExitStack

import concourse.mybir as mybir
from concourse.masks import make_identity

K, T, H, S, T2, NOUT = 512, 4096, 1024, 1024, 2048, 384
FLOPS = 2 * K * H * S * 2 + 2 * H * NOUT * S + 2 * K * NOUT * S

F32 = mybir.dt.float32
BF16 = mybir.dt.bfloat16
I32 = mybir.dt.int32
U32 = mybir.dt.uint32
U16 = mybir.dt.uint16
U8 = mybir.dt.uint8
FP8X4 = mybir.dt.float8_e4m3fn_x4
FP4X4 = mybir.dt.float4_e2m1fn_x4
ACT = mybir.ActivationFunctionType
MULT = mybir.AluOpType.mult

P = 128
PACK = 4
BANK = 512
NBLK = S // P
NT = NOUT // P
PAGES = 3
AHEAD = 3
ADD = mybir.AluOpType.add
FIRST_PIECES = [(0, 2), (2, 4), (4, 8)]
Y_BANKS = (0, 1, 2, 3, 7, 4, 5, 6)
EVEN_PIECES = [(0, 2), (2, 4), (4, 6), (6, 8)]
TAIL_PIECES = [(0, 2), (2, 4), (4, 6), (6, 7), (7, 8)]


def tile_list_wheel_flat_features_kernel(
    tc, tab_words, tab_scales, offs, offs2, offs3, w1, w2_words, w2_scales, wgs, wgt, track, w3, w4_words, w4_scales, out
):
    nc = tc.nc
    with ExitStack() as ctx:
        lists = ctx.enter_context(tc.tile_pool(name="lists", bufs=1))
        keep = ctx.enter_context(tc.tile_pool(name="keep", bufs=1))
        ring = ctx.enter_context(tc.tile_pool(name="ring", bufs=2))
        psum = ctx.enter_context(tc.psum_pool(name="psum", bufs=1))

        def slot(tag, shape, dtype, name):
            return keep.tile(shape, dtype, name=name, tag=tag, align_bytes=64)

        bank_sets = {"mm": (0, 1, 2, 3), "h": (4, 5), "z": (6, 7), "d_tail": (4, 5), "w_tail": (6, 7, 4, 5)}
        turn = {kind: 0 for kind in bank_sets}

        def bank_tile(kind, shape, name, index=None):
            if index is None:
                index = bank_sets[kind][turn[kind] % len(bank_sets[kind])]
                turn[kind] = turn[kind] + 1
            return psum.tile(shape, F32, name=name, tag="bank%d" % index)

        idx = lists.tile([P, S // 16], U16, name="idx")
        idx2 = lists.tile([P, S // 16], U16, name="idx2")
        idx3 = lists.tile([P, S // 16], U16, name="idx3")

        tabs = slot("row0", [P, T], U8, "tabs")
        vs = slot("vs", [P, S], U8, "vs")
        w2w_raw = slot("row1", [P, 2 * H], U8, "w2w_raw")
        w2s_raw = slot("w2s_raw", [P, H], U8, "w2s_raw")
        w2w = slot("w2w", [P, 2 * H], U8, "w2w")
        w2s = slot("w2s", [P, H], U8, "w2s")
        w1b = [slot("w1b%d" % b, [P, PACK, BANK], BF16, "w1b") for b in range(2)]
        w1c = slot("w1c", [P, H], U32, "w1c")
        w1s = slot("w1s", [P, H], U8, "w1s")
        w3b = slot("w3b", [P, NOUT * PACK], BF16, "w3b")
        w3c = slot("w3c", [P, NOUT], U32, "w3c")
        w3s = slot("w3s", [P, NOUT], U8, "w3s")
        pages = {i: slot("page%d" % i, [P, T2], F32, "page") for i in range(1)}
        zc = [slot("zc%d" % b, [P, S], U32, "zc") for b in range(2)]
        zs = [slot("zs%d" % b, [P, S], U8, "zs") for b in range(2)]
        damp = slot("damp", [P, NT, S], F32, "damp")
        ident = slot("ident", [P, P], F32, "ident")

        w1v = w1.rearrange("(p i) r -> p i r", i=PACK)
        trackv = track.rearrange("(b p t) j -> b p t j", b=2, t=PACK)
        outv = out.rearrange("(n p) j -> p n j", p=P)

        nc.sync.dma_start(idx[:], offs)
        nc.sync.dma_start(idx2[:], offs2)
        nc.sync.dma_start(idx3[:], offs3)
        nc.sync.dma_start(w2w_raw[:].bitcast(I32), w2_words[0].bitcast(I32))
        w1raw = {}

        def load_w1(b, tag):
            w1raw[b] = slot(tag, [P, PACK, BANK], F32, "w1raw")
            nc.sync.dma_start(w1raw[b][:], w1v[:, :, b * BANK : (b + 1) * BANK])

        load_w1(0, "wraw")
        nc.vector.memset(tabs[:].bitcast(I32), 0)
        for q in range(4):
            nc.sync.dma_start(tabs[32 * q : 32 * q + 4, :].bitcast(I32), tab_scales[0, 4 * q : 4 * q + 4, :].bitcast(I32))
        ident_first = slot("big0", [P, P], F32, "ident_first")
        make_identity(nc, ident_first[:])
        nc.gpsimd.memset(w2s_raw[:].bitcast(I32), 0)
        for q in range(4):
            nc.gpsimd.dma_start(w2s_raw[32 * q : 32 * q + 4, :].bitcast(I32), w2_scales[0, 4 * q : 4 * q + 4, :].bitcast(I32))
        nc.vector.tensor_copy(ident[:], ident_first[:])
        tabw = slot("big0", [P, T], I32, "tabw")
        nc.sync.dma_start(tabw[:], tab_words[0].rearrange("p t i -> p (t i)").bitcast(I32))
        nc.vector.memset(pages[0][:], 0.0)

        def deal_w2(b):
            words = slice(2 * BANK * b, 2 * BANK * (b + 1))
            nc.vector.tensor_copy(
                w2w[:, words].bitcast(U16).rearrange("p (t q) -> p t q", t=PACK), w2w_raw[:, words].bitcast(U16).rearrange("p (q t) -> p t q", t=PACK)
            )

        def deal_w2_scales(b):
            cols = slice(BANK * b, BANK * (b + 1))
            nc.vector.tensor_copy(w2s[:, cols].rearrange("p (t q) -> p t q", t=PACK), w2s_raw[:, cols].rearrange("p (q t) -> p t q", t=PACK))

        deal_w2(0)
        deal_w2(1)
        wgs_sb = slot("row1", [P, S], F32, "wgs_sb")
        nc.sync.dma_start(wgs_sb[:], wgs)
        nc.vector.tensor_copy(vs[:], tabs[:].indirect(idx[:]))
        deal_w2_scales(0)
        wgt_sb = slot("row0", [P, S], F32, "wgt_sb")
        nc.sync.dma_start(wgt_sb[:], wgt)

        def v_block(c):
            return vw[c // 4][:, (c % 4) * P : (c % 4 + 1) * P].bitcast(FP8X4), vs[:, c * P : (c + 1) * P]

        def quantize_w1(b, t0, t1):
            cols = slice(b * BANK + t0 * P, b * BANK + t1 * P)
            nc.vector.quantize_mx(
                out=w1c[:, cols].bitcast(FP8X4), scales=w1s[:, cols], in_=w1b[b][:, t0:t1, :].rearrange("p t m -> p (t m)")
            )

        def cast_w1(copy, b, ts, qs):
            src = w1raw[b][:].rearrange("p i (q t) -> p q t i", t=PACK)[:, qs, ts, :]
            dst = w1b[b][:].rearrange("p t (q i) -> p q t i", i=PACK)[:, qs, ts, :]
            copy(dst, src)

        h_tiles = {}
        first_tenants = {
            (0, 2): ("page1", None),
            (0, 4): ("wgt_neg", "page2"),
            (2, 0): ("big1", "w4w"),
            (2, 4): ("w4s", None),
        }
        for s in range(1, 4):
            first_tenants[(s + 2, 4)] = ("x%d" % s, None)
        first_tenants[(6, 4)] = ("x4", "x5")

        def staging(tag, n, name):
            if tag is None:
                return ring.tile([P, n, P], F32, name=name, tag=name)
            return slot(tag, [P, n, P], F32, name)

        h_banks = {}

        def sum_h(s, c0, c1):
            n = c1 - c0
            tags = first_tenants.get((s, c0), (None, None))
            cols = slice(s * P, (s + 1) * P)
            strike_bank = bank_tile("mm", [P, n, P], "strike_bank")
            bend_bank = bank_tile("mm", [P, n, P], "bend_bank")
            for cc in range(n):
                codes, scales = v_block(c0 + cc)
                nc.tensor.matmul_mx(
                    out=strike_bank[:, cc, :], lhsT=codes, lhsT_scale=scales,
                    rhs=w1c[:, cols].bitcast(FP8X4), rhs_scale=w1s[:, cols], start=True, stop=True,
                )
            for cc in range(n):
                codes, scales = v_block(c0 + cc)
                nc.tensor.matmul_mx(
                    out=bend_bank[:, cc, :], lhsT=codes, lhsT_scale=scales,
                    rhs=w2w[:, 2 * P * s : 2 * P * (s + 1)].bitcast(FP4X4), rhs_scale=w2s[:, cols], start=True, stop=True,
                )
            strikeT = staging(tags[0], n, "strikeT")
            nc.scalar.activation(strikeT[:], strike_bank[:], ACT.Abs)
            bendT = staging(tags[1], n, "bendT")
            nc.scalar.copy(bendT[:], bend_bank[:])
            hb = bank_tile("h", [P, n, P], "h_bank")
            for cc in range(n):
                nc.tensor.matmul(hb[:, cc, :], strikeT[:, cc, :], ident[:], start=(cc == 0), stop=False, is_transpose=True)
            for cc in range(n):
                nc.tensor.matmul(hb[:, cc, :], bendT[:, cc, :], ident[:], start=False, stop=(cc == n - 1), is_transpose=True)
            h_banks[(s, c0)] = hb

        def copy_h(s, c0, c1):
            if c0 == 0 and s < 6:
                h_tiles[s] = ring.tile([P, S], F32, name="h", tag="h", bufs=AHEAD + 1)
            if c0 == 0 and s >= 6:
                h_tiles[s] = slot("h_last", [P, S], F32, "h")
            nc.scalar.copy(h_tiles[s][:, c0 * P : c1 * P], h_banks[(s, c0)][:].rearrange("p c j -> p (c j)"))

        def make_h(s, c0, c1):
            sum_h(s, c0, c1)
            copy_h(s, c0, c1)

        def make_h_direct(s, c0, c1):
            rows = slice(s * P, (s + 1) * P)
            cols = slice(c0 * P, c1 * P)
            width = (c1 - c0) * P
            strike_bank = bank_tile("mm", [P, width], "strike_bank")
            bend_bank = bank_tile("mm", [P, width], "bend_bank")
            nc.tensor.matmul_mx(
                out=strike_bank[:], lhsT=w1c[:, rows].bitcast(FP8X4), lhsT_scale=w1s[:, rows],
                rhs=vw[0][:, cols].bitcast(FP8X4), rhs_scale=vs[:, cols], start=True, stop=True,
            )
            nc.tensor.matmul_mx(
                out=bend_bank[:], lhsT=w2w[:, 2 * P * s : 2 * P * (s + 1)].bitcast(FP4X4), lhsT_scale=w2s[:, rows],
                rhs=vw[0][:, cols].bitcast(FP8X4), rhs_scale=vs[:, cols], start=True, stop=True,
            )
            strike = slot("late", [P, width], F32, "strike")
            nc.scalar.activation(strike[:], strike_bank[:], ACT.Abs)
            nc.vector.tensor_tensor(h_tiles[s][:, cols], bend_bank[:], strike[:], ADD)

        def put_h(s, c0, c1):
            cols = slice(c0 * P, c1 * P)
            nc.vector.tensor_tensor(pages[s % PAGES][:].indirect(idx2[:, c0 * P // 16 : c1 * P // 16]), h_tiles[s][:, cols], wgs_sb[:, cols], MULT)

        x_tiles = {}

        def pick_x(s, dst, c0, c1):
            cols = slice(c0 * P, c1 * P)
            nc.vector.tensor_tensor(dst, pages[s % PAGES][:].indirect(idx3[:, c0 * P // 16 : c1 * P // 16]), wgt_neg[:, cols], MULT)

        track_tiles = {}

        def load_track(b):
            track_tiles[b] = slot("big%d" % b, [P, PACK, S], F32, "track_sb")
            nc.sync.dma_start(track_tiles[b][:], trackv[b])

        zT = {}

        def distance(b, u, c0, c1, slices, kind):
            n = c1 - c0
            bank = bank_tile(kind, [P, n, slices, P], "d_bank")
            slots = [(cc, e) for e in range(slices) for cc in range(n)]
            for m, (cc, e) in enumerate(slots):
                cols = slice((c0 + cc) * P, (c0 + cc + 1) * P)
                nc.tensor.matmul(bank[:, cc, e, :], track_tiles[b][:, 2 * u + e, cols], ident[:], start=(m == 0), stop=False, is_transpose=True)
            for m, (cc, e) in enumerate(slots):
                cols = slice((c0 + cc) * P, (c0 + cc + 1) * P)
                nc.tensor.matmul(
                    bank[:, cc, e, :], x_tiles[PACK * b + 2 * u + e][:, cols], ident[:], start=False, stop=(m == len(slots) - 1), is_transpose=True
                )
            zt = ring.tile([P, n * 2 * P], BF16, name="zT", tag="zT%d%d" % (u, slices), bufs=(4 if slices == 2 else 2))
            src = bank[:].rearrange("j c e p -> j c p e")
            if slices == 1:
                src = src.to_broadcast([P, n, P, 2])
            nc.scalar.activation(zt[:].rearrange("j (c p e) -> j c p e", c=n, e=2), src, ACT.Abs)
            for cc in range(n):
                zT[(b, u, c0 + cc)] = zt[:].bitcast(F32)[:, cc * P : (cc + 1) * P]

        def turn_back(b, c0, c1, kind):
            n = c1 - c0
            bank = bank_tile(kind, [P, n, 2, P], "w_bank")
            for u in range(2):
                for cc in range(n):
                    nc.tensor.transpose(bank[:, cc, u, :], zT[(b, u, c0 + cc)], ident[:])
            zq = ring.tile([P, n * P * PACK], BF16, name="zq", tag="zq", bufs=5, align_bytes=64)
            nc.scalar.copy(zq[:].bitcast(F32).rearrange("p (c j u) -> p c j u", c=n, u=2), bank[:].rearrange("p c u j -> p c j u"))
            return zq

        def quantize_z(b, zq, c0, c1):
            cols = slice(c0 * P, c1 * P)
            nc.vector.quantize_mx(out=zc[b][:, cols].bitcast(FP8X4), scales=zs[b][:, cols], in_=zq[:])

        def prepare_w3():
            raw = slot("late", [P, PACK, NOUT], F32, "w3raw")
            nc.sync.dma_start(raw[:], w3.rearrange("(p i) n -> p i n", i=PACK))
            for n in range(NT):
                cols = slice(n * P, (n + 1) * P)
                nc.scalar.copy(w3b[:].rearrange("p (n i) -> p n i", i=PACK)[:, cols, :], raw[:].rearrange("p i n -> p n i")[:, cols, :])
            for c0, c1 in ((0, 256), (256, NOUT)):
                nc.vector.quantize_mx(out=w3c[:, c0:c1].bitcast(FP8X4), scales=w3s[:, c0:c1], in_=w3b[:, PACK * c0 : PACK * c1])

        def damping(n):
            cols = slice(n * P, (n + 1) * P)
            for half in range(2):
                bank = bank_tile("mm", [P, BANK], "b_bank")
                nc.tensor.matmul_mx(
                    out=bank[:], lhsT=w3c[:, cols].bitcast(FP8X4), lhsT_scale=w3s[:, cols],
                    rhs=vw[half][:].bitcast(FP8X4), rhs_scale=vs[:, half * BANK : (half + 1) * BANK], start=True, stop=True,
                )
                nc.scalar.activation(damp[:, n, half * BANK : (half + 1) * BANK], bank[:], ACT.Square)
            nc.scalar.activation(damp[:, n, :], damp[:, n, :], ACT.Abs_reciprocal_sqrt, bias=1.0)
            nc.scalar.activation(damp[:, n, :], damp[:, n, :], ACT.Square)

        def y_passes(bank, a, n0, n1, c0, c1):
            cols = slice(c0 * P, c1 * P)
            for n in range(n0, n1):
                nc.tensor.matmul_mx(
                    out=bank[:, n - n0, :], lhsT=w4w[:, a, n * P : (n + 1) * P].bitcast(FP8X4), lhsT_scale=w4s[:, a, n * P : (n + 1) * P],
                    rhs=zc[a][:, cols].bitcast(FP8X4), rhs_scale=zs[a][:, cols], start=(a == 0 and n == n0), stop=(a == 1 and n == n1 - 1),
                )

        cast_w1(nc.scalar.copy, 0, slice(0, PACK), slice(0, P))
        quantize_w1(0, 0, PACK)
        deal_w2_scales(1)
        vw = [slot(tag, [P, BANK], U32, "vw") for tag in ("w1b0", "w2s_raw")]
        for half in range(2):
            nc.vector.tensor_copy(vw[half][:], tabw[:].bitcast(U32).indirect(idx[:, 32 * half : 32 * half + 32]))
        h_tiles[0] = ring.tile([P, S], F32, name="h", tag="h", bufs=AHEAD + 1)
        make_h_direct(0, *FIRST_PIECES[0])
        for c0, c1 in FIRST_PIECES[1:]:
            make_h(0, c0, c1)
        make_h(1, 0, 4)
        make_h(1, 4, NBLK)
        wgt_neg = slot("wgt_neg", [P, S], F32, "wgt_neg")
        nc.scalar.activation(wgt_neg[:], wgt_sb[:], ACT.Copy, scale=-1.0)
        for i in range(1, PAGES):
            pages[i] = slot("page%d" % i, [P, T2], F32, "page")
            nc.gpsimd.memset(pages[i][:], 0.0)
        load_track(0)

        last = 2 * PACK - 1
        load_w1(1, "late")
        for q0 in range(0, P, 32):
            cast_w1(nc.scalar.copy, 1, slice(0, PACK), slice(q0, q0 + 32))
        quantize_w1(1, 0, PACK)
        for s in range(2, AHEAD):
            make_h(s, 0, 4)
            make_h(s, 4, NBLK)
        for c0, c1 in FIRST_PIECES:
            put_h(0, c0, c1)
        for s in range(last):
            b, t = divmod(s, PACK)
            if s + AHEAD < last:
                make_h(s + AHEAD, 0, 4)
                make_h(s + AHEAD, 4, NBLK)
            if s + AHEAD == last:
                sum_h(last, 0, 4)
                sum_h(last, 4, NBLK)
            if s == 1:
                prepare_w3()
                load_track(1)
                w4w = slot("w4w", [P, 2, NOUT], I32, "w4w")
                w4s = slot("w4s", [P, 2, NOUT], U8, "w4s")
                nc.gpsimd.memset(w4s[:].rearrange("p a n -> p (a n)").bitcast(I32), 0)
                nc.sync.dma_start(w4w[:], w4_words.rearrange("a p n i -> p a (n i)").bitcast(I32))
                for q in range(4):
                    nc.sync.dma_start(
                        w4s[32 * q : 32 * q + 4, :, :].bitcast(I32), w4_scales[:, 4 * q : 4 * q + 4, :].rearrange("a r n -> r a n").bitcast(I32)
                    )
            if 2 <= s < 2 + NT:
                damping(s - 2)
            if s == 1:
                put_h(1, 0, NBLK)
            if 1 <= s < last - 2:
                put_h(s + 1, 0, NBLK)
            if s == last - 1:
                put_h(s, 0, NBLK)
                copy_h(last, 0, 4)
                copy_h(last, 4, NBLK)
            x_tiles[s] = slot("x%d" % s, [P, S], F32, "xneg")
            pick_x(s, x_tiles[s][:], 0, NBLK)
            if t % 2 == 1:
                for c0, c1 in EVEN_PIECES:
                    distance(b, t // 2, c0, c1, 2, "z")
                    if t == PACK - 1:
                        quantize_z(b, turn_back(b, c0, c1, "z"), c0, c1)

        zq_tail = {}
        distance(1, 1, 0, 4, 1, "d_tail")
        distance(1, 1, 4, NBLK, 1, "d_tail")
        for c0, c1 in TAIL_PIECES:
            zq_tail[c0] = turn_back(1, c0, c1, "w_tail")
        put_h(last, 0, NBLK)
        y_banks = {}
        index = 0
        for c0, c1 in TAIL_PIECES:
            width = (c1 - c0) * P
            per_bank = BANK // width
            y_banks[c0] = []
            for n0 in range(0, NT, per_bank):
                n1 = min(NT, n0 + per_bank)
                bank = bank_tile("mm", [P, n1 - n0, width], "y_bank", Y_BANKS[index])
                index = index + 1
                y_passes(bank, 0, n0, n1, c0, c1)
                y_banks[c0].append((bank, n0, n1))
        for c0, c1 in TAIL_PIECES:
            cols = slice(c0 * P, c1 * P)
            width = (c1 - c0) * P
            xl = ring.tile([P, width], F32, name="x_last", tag="x_last", bufs=5)
            pick_x(last, xl[:], c0, c1)
            dl = ring.tile([P, width], F32, name="d_last", tag="d_last", bufs=5)
            nc.vector.tensor_tensor(dl[:], xl[:], track_tiles[1][:, PACK - 1, cols], ADD)
            nc.scalar.activation(zq_tail[c0][:].rearrange("p (j t) -> p j t", t=PACK)[:, :, PACK - 1], dl[:], ACT.Abs)
        for c0, c1 in TAIL_PIECES:
            cols = slice(c0 * P, c1 * P)
            quantize_z(1, zq_tail[c0], c0, c1)
            res = ring.tile([P, NT, (c1 - c0) * P], F32, name="res", tag="res", bufs=4)
            for bank, n0, n1 in y_banks[c0]:
                y_passes(bank, 1, n0, n1, c0, c1)
                nc.vector.tensor_tensor(res[:, n0:n1, :], bank[:], damp[:, n0:n1, cols], MULT)
            nc.sync.dma_start(outv[:, :, cols], res[:])
